import numpy as np
import ml_dtypes


def mxq(x, axis, fmt="e4m3"):
    dtype, down = {"e4m3": (ml_dtypes.float8_e4m3fn, 7), "e5m2": (ml_dtypes.float8_e5m2, 14)}[fmt]
    v = np.moveaxis(np.asarray(x, np.float32).astype(ml_dtypes.bfloat16).astype(np.float64), axis, -1)
    blocks = v.reshape(v.shape[:-1] + (-1, 32))
    amax = np.abs(blocks).max(-1, keepdims=True)
    byte = np.maximum(np.where(amax > 0, np.frexp(amax)[1] - 1 + 127, 0) - down, 1)
    scale = np.exp2(byte - 127.0)
    codes = (blocks / scale).astype(np.float32).astype(dtype).astype(np.float64)
    return np.moveaxis((codes * scale).reshape(v.shape), -1, axis)


WIDE = False


def mx_kscale(k):
    if not WIDE:
        return np.ones(k)
    levels = np.array([10, -10, 5, -5, 0])
    if k % 512:
        return np.exp2(np.random.permutation(np.resize(levels, k // 32))).repeat(32)
    a = np.empty((k // 512, 16))
    for p in range(k // 512):
        a[p, :8] = np.random.permutation(np.resize(levels, 8))
        for g in range(8):
            far = levels[np.abs(levels - a[p, g]) >= 10]
            a[p, g + 8] = far[np.random.randint(len(far))]
    return np.exp2(a.ravel()).repeat(32)


BF16 = ml_dtypes.bfloat16


def bf(x):
    return np.asarray(x, np.float32).astype(BF16)


def f64(x):
    return np.asarray(x).astype(np.float64)


E2M1 = np.array([0.0, 0.5, 1.0, 1.5, 2.0, 3.0, 4.0, 6.0, -0.0, -0.5, -1.0, -1.5, -2.0, -3.0, -4.0, -6.0])


def pack_weight(w, fmt):
    k, n = w.shape
    w = f64(bf(w)).reshape(k // 32, 32, n)
    amax = np.abs(w).max(1)
    if fmt == "e4m3":
        byte = np.frexp(amax)[1] - 1 + 127 - 7
    else:
        mant, ex = np.frexp(amax / 6.0)
        byte = np.where(mant > 0.5, ex, ex - 1) + 127
    byte = np.clip(np.where(amax > 0, byte, 1), 1, 254)
    scaled = (w * np.exp2(127.0 - byte)[:, None, :]).reshape(k, n).astype(np.float32)
    by_word = np.ascontiguousarray(scaled.reshape(k // 512, 128, 4, n).transpose(0, 1, 3, 2))
    if fmt == "e4m3":
        words = by_word.astype(ml_dtypes.float8_e4m3fn).view(np.uint8)
    else:
        c = by_word.astype(ml_dtypes.float4_e2m1fn).view(np.uint8) & 0xF
        words = c[..., 0::2] | (c[..., 1::2] << 4)
    return np.ascontiguousarray(words), np.ascontiguousarray(byte.astype(np.uint8).reshape(k // 512, 16, n))


def unpack_weight(words, scales, fmt):
    g, p, n, _ = words.shape
    if fmt == "e4m3":
        vals = np.ascontiguousarray(words).view(ml_dtypes.float8_e4m3fn).astype(np.float64)
    else:
        nib = np.empty((g, p, n, 4), np.uint8)
        nib[..., 0::2] = words & 0xF
        nib[..., 1::2] = words >> 4
        vals = E2M1[nib]
    vals = vals * np.repeat(np.exp2(scales.astype(np.float64) - 127.0), 8, axis=1)[..., None]
    return vals.transpose(0, 1, 3, 2).reshape(g * 512, n)
def pack4(w):
    words, scales = pack_weight(w, "e2m1")
    return words.reshape(words.shape[0], 128, -1), scales


def unpack4(words, scales):
    return unpack_weight(words.reshape(words.shape[0], 128, -1, 2), scales, "e2m1")


def planes(Y):
    n, m = Y.shape
    b = f64(bf(Y)).reshape(n // 32, 32, m)
    amax = np.abs(b).max(1)
    byte = np.clip(np.where(amax > 0, np.frexp(amax)[1] - 1 + 127 - 7, 1), 1, 254)
    codes = (b * np.exp2(127.0 - byte)[:, None, :]).reshape(n, m).astype(np.float32).astype(ml_dtypes.float8_e4m3fn).view(np.uint8)
    words = codes.reshape(n // 512, 128, 4, m).transpose(0, 1, 3, 2)
    return np.ascontiguousarray(words), np.ascontiguousarray(byte.astype(np.uint8).reshape(n // 512, 16, m))


S, NX, NV, J = 4, 1024, 512, 512
VMAX, SCREEN = 2.0, 0.125
LAM = SCREEN * NX

def screened_inverse(eps, lam):
    eye = np.eye(NX)
    flux = eps[:, None] * (eye - np.roll(eye, 1, axis=1))
    return 2.0 * LAM ** -1.5 * np.linalg.inv(flux - np.roll(flux, 1, axis=0) + eye / lam ** 2)

def setup_inputs():
    s = mx_kscale(S * NV)
    t = mx_kscale(S * NX)
    envelope = np.exp(-0.5 * np.linspace(-VMAX, VMAX, NV) ** 2)
    delta_f = np.random.randn(S, NX, NV) * envelope * s.reshape(S, 1, NV) * t.reshape(S, NX, 1)
    W = np.random.randn(S * NV, J) / np.sqrt(np.sum(envelope ** 2)) / s[:, None]
    eps = np.exp(0.3 * np.random.randn(S, NX))
    lam = LAM * np.exp(0.2 * np.random.randn(S))
    H = np.concatenate([screened_inverse(eps[a], lam[a]) for a in range(S)], axis=0) / t[:, None]
    w_words, w_scales = pack4(W)
    h_words, h_scales = pack4(H)
    return {"delta_f": bf(delta_f), "w_words": w_words, "w_scales": w_scales,
            "rho_bg": bf(0.5 * np.random.randn(S, NX) * t.reshape(S, NX)),
            "h_words": h_words, "h_scales": h_scales,
            "phi_ext": bf(0.5 * np.random.randn(S, NX)),
            "gain": bf(np.exp(0.8 * np.random.randn(S, NX)))}

def reference(delta_f, w_words, w_scales, rho_bg, h_words, h_scales, phi_ext, gain):
    W = unpack4(w_words, w_scales).reshape(S, NV, J)
    H = unpack4(h_words, h_scales).reshape(S, NX, NX)
    rho = (mxq(f64(delta_f), 2, "e4m3") @ W) + f64(rho_bg)[:, :, None]
    phi = mxq(rho, 1, "e4m3").swapaxes(1, 2) @ H
    y = (phi + f64(phi_ext)[:, None, :]) * f64(gain)[:, None, :]
    Y = y.reshape(S * J, NX).T
    words, scales = planes(Y)
    return y, words, scales

@@ -1,0 +1,332 @@
+from contextlib import ExitStack
+
+import concourse.mybir as mybir
+from concourse.masks import make_identity
+
+S, NX, NV, J = 4, 1024, 512, 512
+FLOPS = 2 * S * NX * NV * J + 2 * S * J * NX * NX
+
+F32 = mybir.dt.float32
+BF16 = mybir.dt.bfloat16
+I32 = mybir.dt.int32
+U32 = mybir.dt.uint32
+U8 = mybir.dt.uint8
+FP8X4 = mybir.dt.float8_e4m3fn_x4
+FP4X4 = mybir.dt.float4_e2m1fn_x4
+ADD = mybir.AluOpType.add
+MULT = mybir.AluOpType.mult
+
+P = 128
+GROUPS = 2 * S
+TILES = 4 * S
+TAIL = 11
+
+
+def tile_weighted_density_screened_poisson_k7_kernel(
+    tc, delta_f, w_words, w_scales, rho_bg, h_words, h_scales, phi_ext, gain, out_0, out_1, out_2
+):
+    nc = tc.nc
+    with ExitStack() as ctx:
+        keep = ctx.enter_context(tc.tile_pool(name="keep", bufs=1))
+        work = ctx.enter_context(tc.tile_pool(name="work", bufs=2))
+        psum = ctx.enter_context(tc.psum_pool(name="psum", bufs=2))
+        ctx.enter_context(tc.manual_schedule())
+
+        ident = keep.tile([P, P], F32, name="ident", align_bytes=64)
+        w_sb = keep.tile([P, S, 2 * J], U8, name="w_sb", align_bytes=64)
+        w_sc = keep.tile([P, S, J], U8, name="w_sc", align_bytes=64)
+        h_sb = keep.tile([P, GROUPS, 2 * NX], U8, name="h_sb", align_bytes=64)
+        h_sc = keep.tile([P, GROUPS, NX], U8, name="h_sc", align_bytes=64)
+        bg = keep.tile([P, GROUPS, 4], BF16, name="bg", align_bytes=64)
+        ext_bc = keep.tile([P, S, NX], BF16, name="ext_bc", align_bytes=64)
+        gain_bc = keep.tile([P, S, NX], BF16, name="gain_bc", align_bytes=64)
+        y_codes = keep.tile([P, 2, S * J], U32, name="y_codes", align_bytes=64)
+        y_sc = keep.tile([P, 2, S * J], U8, name="y_sc", align_bytes=64)
+
+        make_identity(nc, ident[:])
+        nc.vector.memset(w_sc[:].rearrange("p a n -> p (a n)").bitcast(I32), 0)
+        nc.vector.memset(h_sc[:].rearrange("p a n -> p (a n)").bitcast(I32), 0)
+
+        df = {}
+
+        def load_df(h, pieces):
+            a, g = divmod(h, 2)
+            df[h] = work.tile([P, 4, NV], BF16, name="df", bufs=5, align_bytes=64)
+            src = delta_f[a, 512 * g : 512 * (g + 1), :].rearrange("(p t) v -> p t v", t=4)
+            step = 4 // pieces
+            for t0 in range(0, 4, step):
+                nc.sync.dma_start(out=df[h][:, t0 : t0 + step, :], in_=src[:, t0 : t0 + step, :])
+
+        def load_scales(engine, plane, src):
+            for q in range(4):
+                engine.dma_start(
+                    out=plane[32 * q : 32 * q + 4, :, :].bitcast(I32),
+                    in_=src[:, 4 * q : 4 * q + 4, :].rearrange("g r n -> r g n").bitcast(I32),
+                )
+
+        def load_words(dst, src, g0, g1):
+            nc.sync.dma_start(
+                out=dst[:, g0:g1, :].bitcast(I32),
+                in_=src[g0:g1, :, :].rearrange("g p n -> p g n").bitcast(I32),
+            )
+
+        def load_rows(a):
+            nc.sync.dma_start(out=ext_bc[:, a, :], in_=phi_ext[a, :].partition_broadcast(P))
+            nc.sync.dma_start(out=gain_bc[:, a, :], in_=gain[a, :].partition_broadcast(P))
+
+        load_scales(nc.scalar, w_sc, w_scales)
+        load_df(0, 2)
+        load_words(w_sb, w_words, 0, 1)
+        nc.sync.dma_start(out=bg[:], in_=rho_bg.rearrange("a (g p t) -> p (a g) t", g=2, t=4))
+        load_df(1, 1)
+        load_df(2, 1)
+        load_scales(nc.sync, h_sc, h_scales)
+        load_words(h_sb, h_words, 0, 2)
+        load_words(w_sb, w_words, 1, S)
+        load_df(3, 1)
+        load_rows(0)
+        load_df(4, 1)
+
+        def late_loads(step):
+            if step == -7:
+                load_words(h_sb, h_words, 2, 4)
+            if step == -7:
+                load_df(5, 1)
+                load_rows(1)
+            if step == -5:
+                load_df(6, 1)
+                load_words(h_sb, h_words, 4, 6)
+            if step == -3:
+                load_df(7, 1)
+                load_rows(2)
+                load_words(h_sb, h_words, 6, 8)
+                load_rows(3)
+
+        q_in, q_codes, q_sc = {}, {}, {}
+
+        def staging(k):
+            if k not in q_in:
+                q_in[k] = work.tile([P, 2, 2048], BF16, name="q_in", bufs=3, align_bytes=64)
+            return q_in[k]
+
+        def turn_df(h, half):
+            bank = psum.tile([P, 2, 2, P], F32, name="turn", bufs=2)
+            for tl in range(2):
+                words = df[h][:, 2 * half + tl, :].bitcast(F32)
+                for u in range(2):
+                    nc.tensor.transpose(bank[:, tl, u, :], words[:, u:256:2], ident[:])
+            return bank
+
+        def copy_df(h, half, bank):
+            dst = staging(h - 2)[:, 0, 1024 * half : 1024 * (half + 1)].bitcast(F32)
+            nc.scalar.copy(
+                out=dst.rearrange("p (t r u) -> p t r u", t=2, u=2),
+                in_=bank[:].rearrange("p t u r -> p t r u"),
+            )
+
+        def quantize_pair(k):
+            q_codes[k] = work.tile([P, 2, 512], U32, name="q_codes", bufs=5, align_bytes=64)
+            q_sc[k] = work.tile([P, 2, 512], U8, name="q_sc", bufs=5, align_bytes=64)
+            lo = 0 if k + 2 < GROUPS else 1
+            hi = 2 if k >= 0 else 1
+            nc.vector.quantize_mx(
+                out=q_codes[k][:, lo:hi, :].rearrange("p s n -> p (s n)").bitcast(FP8X4),
+                scales=q_sc[k][:, lo:hi, :].rearrange("p s n -> p (s n)"),
+                in_=q_in[k][:, lo:hi, :].rearrange("p s n -> p (s n)"),
+            )
+
+        rho_banks, phi_banks, sums, ys, ybf, yt = {}, {}, {}, {}, {}, {}
+
+        def density(h, jc):
+            a = h // 2
+            bank = psum.tile([P, 512], F32, name="acc", bufs=6)
+            rho_banks[h, jc] = bank
+            for t in range(4):
+                cols = slice(P * t, P * (t + 1))
+                nc.tensor.matmul_mx(
+                    out=bank[:, cols],
+                    lhsT=q_codes[h - 2][:, 0, cols].bitcast(FP8X4),
+                    lhsT_scale=q_sc[h - 2][:, 0, cols],
+                    rhs=w_sb[:, a, 2 * P * jc : 2 * P * (jc + 1)].bitcast(FP4X4),
+                    rhs_scale=w_sc[:, a, P * jc : P * (jc + 1)],
+                    start=True,
+                    stop=True,
+                )
+
+        def add_background(h, jc):
+            nc.vector.tensor_tensor(
+                out=staging(h)[:, 1, 512 * jc : 512 * (jc + 1)].rearrange("p (n t) -> p n t", t=4),
+                in0=rho_banks[h, jc][:].rearrange("p (t n) -> p n t", t=4),
+                in1=bg[:, h, :].unsqueeze(1).to_broadcast([P, P, 4]),
+                op=ADD,
+            )
+
+        def potential(s, zh):
+            a, jt = divmod(s, 4)
+            bank = psum.tile([P, 512], F32, name="acc", bufs=6)
+            phi_banks[s, zh] = bank
+            cols = slice(P * jt, P * (jt + 1))
+            for g in range(2):
+                h = 2 * a + g
+                nc.tensor.matmul_mx(
+                    out=bank[:],
+                    lhsT=q_codes[h][:, 1, cols].bitcast(FP8X4),
+                    lhsT_scale=q_sc[h][:, 1, cols],
+                    rhs=h_sb[:, h, 1024 * zh : 1024 * (zh + 1)].bitcast(FP4X4),
+                    rhs_scale=h_sc[:, h, 512 * zh : 512 * (zh + 1)],
+                    start=(g == 0),
+                    stop=(g == 1),
+                )
+
+        def add_external(s, zh):
+            a = s // 4
+            if zh == 0:
+                sums[s] = work.tile([P, NX], F32, name="sums", bufs=3, align_bytes=64)
+            cols = slice(512 * zh, 512 * (zh + 1))
+            nc.vector.tensor_tensor(out=sums[s][:, cols], in0=phi_banks[s, zh][:], in1=ext_bc[:, a, cols], op=ADD)
+
+        def apply_gain(s, z0, z1, engine):
+            a = s // 4
+            if z0 == 0:
+                ys[s] = work.tile([P, NX], F32, name="y", bufs=10, align_bytes=64)
+            engine.tensor_tensor(out=ys[s][:, z0:z1], in0=sums[s][:, z0:z1], in1=gain_bc[:, a, z0:z1], op=MULT)
+
+        def store_y(s, z0, z1):
+            a, jt = divmod(s, 4)
+            nc.sync.dma_start(out=out_0[a, P * jt : P * (jt + 1), z0:z1], in_=ys[s][:, z0:z1])
+
+        def round_y(s, zh):
+            ybf[s, zh] = work.tile([P, 2, P, 2], BF16, name="ybf", bufs=6, align_bytes=64)
+            nc.scalar.copy(
+                out=ybf[s, zh][:],
+                in_=ys[s][:, 512 * zh : 512 * (zh + 1)].rearrange("p (m u e) -> p u m e", u=2, e=2),
+            )
+
+        def turn_y(s, halves):
+            bank = psum.tile([P, 2, 2, P], F32, name="turn", bufs=2)
+            for zh in halves:
+                for u in range(2):
+                    words = ybf[s, zh][:, u, :, :].rearrange("p m e -> p (m e)").bitcast(F32)
+                    nc.tensor.transpose(bank[:, zh, u, :], words, ident[:])
+            return bank
+
+        def copy_y(s, halves, bank):
+            a, jt = divmod(s, 4)
+            if a not in yt:
+                yt[a] = work.tile([P, 2, 2048], BF16, name="yt", bufs=2, align_bytes=64)
+            g0, g1 = halves[0], halves[-1] + 1
+            dst = yt[a][:, g0:g1, 512 * jt : 512 * (jt + 1)].bitcast(F32)
+            nc.scalar.copy(
+                out=dst.rearrange("p g (r u) -> p g r u", u=2),
+                in_=bank[:, g0:g1, :, :].rearrange("p g u r -> p g r u"),
+            )
+
+        def quantize_y(a, g, j0, j1):
+            cols = slice(J * a + j0, J * a + j1)
+            nc.vector.quantize_mx(
+                out=y_codes[:, g, cols].bitcast(FP8X4), scales=y_sc[:, g, cols], in_=yt[a][:, g, 4 * j0 : 4 * j1]
+            )
+            nc.sync.dma_start(
+                out=out_1[g, :, cols, :].rearrange("p m t -> p (m t)").bitcast(I32),
+                in_=y_codes[:, g, cols].bitcast(I32),
+            )
+
+        def store_scales(engines, m0, m1):
+            for q in range(4):
+                engines[q % len(engines)].dma_start(
+                    out=out_2[:, 4 * q : 4 * q + 4, m0:m1].rearrange("g r m -> r g m").bitcast(I32),
+                    in_=y_sc[32 * q : 32 * q + 4, :, m0:m1].bitcast(I32),
+                )
+
+        def quantize_step(step):
+            if step % 2 and -2 <= (step + 3) // 2 < GROUPS:
+                quantize_pair((step + 3) // 2)
+            if step in (6, 10, 13):
+                quantize_y((step - 5) // 4, 0, 0, J)
+            if step in (8, 12, 14):
+                quantize_y((step - 6) // 4 if step > 8 else 0, 1, 0, J)
+            if step == 15:
+                store_scales([nc.sync], 0, 3 * J)
+                quantize_y(3, 0, 0, 256)
+                quantize_y(3, 1, 0, 256)
+
+        def transposes(step):
+            h, half = divmod(step + 9, 2)
+            jobs = []
+            if h < GROUPS:
+                jobs.append((copy_df, h, half, turn_df(h, half)))
+            todo = []
+            if 0 <= step - 2 and step <= TAIL + 1:
+                todo.append(step - 2)
+            if TAIL + 1 <= step:
+                todo.append(step - 1)
+            for s in todo:
+                jobs.append((copy_y, s, (0, 1), turn_y(s, (0, 1))))
+            for fn, x, part, bank in jobs:
+                fn(x, part, bank)
+
+        def products(step):
+            nxt = step + 1
+            h, first = divmod(nxt + 5, 2)
+            for i in range(2):
+                if 0 <= nxt < TILES:
+                    potential(nxt, i)
+                if 0 <= h < GROUPS:
+                    density(h, 2 * first + i)
+
+        for step in range(-9, TILES):
+            late_loads(step)
+            if step >= 1:
+                round_y(step - 1, 0)
+                round_y(step - 1, 1)
+                store_y(step - 1, 0, NX)
+            early_turn = -4 < step <= TAIL
+            if early_turn:
+                transposes(step)
+            h, first = divmod(step + 5, 2)
+            has_rho = 0 <= h < GROUPS
+            if step == TILES - 1:
+                add_external(step, 0)
+                add_external(step, 1)
+                apply_gain(step, 0, 512, nc.vector)
+                apply_gain(step, 512, NX, nc.vector)
+                quantize_step(step)
+            elif step >= TAIL:
+                add_external(step, 0)
+                add_external(step, 1)
+                apply_gain(step, 0, 520, nc.vector)
+                apply_gain(step, 512, NX, nc.gpsimd)
+                quantize_step(step)
+            elif step >= 0:
+                add_external(step, 0)
+                apply_gain(step, 0, 512, nc.gpsimd)
+                quantize_step(step)
+                add_background(h, 2 * first)
+                add_external(step, 1)
+                apply_gain(step, 512, NX, nc.gpsimd)
+                add_background(h, 2 * first + 1)
+            elif step == -5:
+                add_background(h, 0)
+                add_background(h, 1)
+                quantize_step(step)
+            else:
+                if has_rho:
+                    add_background(h, 2 * first)
+                quantize_step(step)
+                if has_rho:
+                    add_background(h, 2 * first + 1)
+            products(step)
+            if not early_turn:
+                transposes(step)
+
+        last = TILES - 1
+        quantize_y(3, 0, 256, 384)
+        quantize_y(3, 1, 256, 384)
+        for zh in range(2):
+            round_y(last, zh)
+            store_y(last, 512 * zh, 512 * (zh + 1))
+        for zh in range(2):
+            copy_y(last, (zh,), turn_y(last, (zh,)))
+        for zh in range(2):
+            quantize_y(3, zh, 384, 512)
+        store_scales([nc.scalar, nc.sync], 3 * J, 4 * J)

@@ -37,13 +37,17 @@ def tile_weighted_density_screened_poisson_k7_kernel(
         w_sc = keep.tile([P, S, J], U8, name="w_sc", align_bytes=64)
         h_sb = keep.tile([P, GROUPS, 2 * NX], U8, name="h_sb", align_bytes=64)
         h_sc = keep.tile([P, GROUPS, NX], U8, name="h_sc", align_bytes=64)
-        bg = keep.tile([P, GROUPS, 4], BF16, name="bg", align_bytes=64)
+        bg = keep.tile([P, GROUPS, 4], F32, name="bg", align_bytes=64)
+        ident_bf = keep.tile([P, P], BF16, name="ident_bf", align_bytes=64)
+        rows = keep.tile([P, NX], BF16, name="rows", align_bytes=64)
         ext_bc = keep.tile([P, S, NX], BF16, name="ext_bc", align_bytes=64)
         gain_bc = keep.tile([P, S, NX], BF16, name="gain_bc", align_bytes=64)
         y_codes = keep.tile([P, 2, S * J], U32, name="y_codes", align_bytes=64)
         y_sc = keep.tile([P, 2, S * J], U8, name="y_sc", align_bytes=64)
 
         make_identity(nc, ident[:])
+        make_identity(nc, ident_bf[:])
+        nc.vector.memset(rows[:].bitcast(I32), 0)
         nc.vector.memset(w_sc[:].rearrange("p a n -> p (a n)").bitcast(I32), 0)
         nc.vector.memset(h_sc[:].rearrange("p a n -> p (a n)").bitcast(I32), 0)
 
@@ -57,11 +61,11 @@ def tile_weighted_density_screened_poisson_k7_kernel(
             for t0 in range(0, 4, step):
                 nc.sync.dma_start(out=df[h][:, t0 : t0 + step, :], in_=src[:, t0 : t0 + step, :])
 
-        def load_scales(engine, plane, src):
+        def load_scales(engine, plane, src, g0, g1):
             for q in range(4):
                 engine.dma_start(
-                    out=plane[32 * q : 32 * q + 4, :, :].bitcast(I32),
-                    in_=src[:, 4 * q : 4 * q + 4, :].rearrange("g r n -> r g n").bitcast(I32),
+                    out=plane[32 * q : 32 * q + 4, g0:g1, :].bitcast(I32),
+                    in_=src[g0:g1, 4 * q : 4 * q + 4, :].rearrange("g r n -> r g n").bitcast(I32),
                 )
 
         def load_words(dst, src, g0, g1):
@@ -70,37 +74,66 @@ def tile_weighted_density_screened_poisson_k7_kernel(
                 in_=src[g0:g1, :, :].rearrange("g p n -> p g n").bitcast(I32),
             )
 
-        def load_rows(a):
-            nc.sync.dma_start(out=ext_bc[:, a, :], in_=phi_ext[a, :].partition_broadcast(P))
-            nc.sync.dma_start(out=gain_bc[:, a, :], in_=gain[a, :].partition_broadcast(P))
-
-        load_scales(nc.scalar, w_sc, w_scales)
+        nc.scalar.dma_start(out=rows[2 * S : 3 * S, :], in_=rho_bg)
+        load_scales(nc.scalar, w_sc, w_scales, 0, S)
+        nc.scalar.dma_start(out=rows[0:S, :], in_=phi_ext)
+        nc.scalar.dma_start(out=rows[S : 2 * S, :], in_=gain)
         load_df(0, 2)
         load_words(w_sb, w_words, 0, 1)
-        nc.sync.dma_start(out=bg[:], in_=rho_bg.rearrange("a (g p t) -> p (a g) t", g=2, t=4))
         load_df(1, 1)
         load_df(2, 1)
-        load_scales(nc.sync, h_sc, h_scales)
+        load_scales(nc.sync, h_sc, h_scales, 0, 2)
         load_words(h_sb, h_words, 0, 2)
         load_words(w_sb, w_words, 1, S)
         load_df(3, 1)
-        load_rows(0)
         load_df(4, 1)
+        load_scales(nc.sync, h_sc, h_scales, 2, GROUPS)
 
         def late_loads(step):
             if step == -7:
-                load_words(h_sb, h_words, 2, 4)
-            if step == -7:
                 load_df(5, 1)
-                load_rows(1)
+                load_words(h_sb, h_words, 2, 4)
             if step == -5:
                 load_df(6, 1)
                 load_words(h_sb, h_words, 4, 6)
             if step == -3:
                 load_df(7, 1)
-                load_rows(2)
                 load_words(h_sb, h_words, 6, 8)
-                load_rows(3)
+
+        def spread_background():
+            bank = psum.tile([P, 2, 4, S], F32, name="acc", bufs=6)
+            for g in range(2):
+                for t in range(4):
+                    nc.tensor.matmul(
+                        out=bank[:, g, t, :],
+                        lhsT=rows[:, 512 * g + t : 512 * (g + 1) : 4],
+                        rhs=ident_bf[:, 2 * S : 3 * S],
+                        start=True,
+                        stop=True,
+                    )
+            nc.scalar.copy(
+                out=bg[:].rearrange("p (a g) t -> p a g t", g=2), in_=bank[:].rearrange("p g t a -> p a g t")
+            )
+
+        def spread_row(r, dst):
+            bank = psum.tile([P, NX], BF16, name="acc", bufs=6)
+            for zh in range(2):
+                cols = slice(512 * zh, 512 * (zh + 1))
+                nc.tensor.matmul(
+                    out=bank[:, cols],
+                    lhsT=ident_bf[:, r : r + 1].to_broadcast([P, P]),
+                    rhs=rows[:, cols],
+                    start=True,
+                    stop=True,
+                )
+            nc.scalar.copy(out=dst, in_=bank[:])
+
+        def spread(step):
+            if step == -8:
+                spread_background()
+            if -7 <= step < 1:
+                a, which = divmod(step + 7, 2)
+                spread_row(a + S * which, (ext_bc, gain_bc)[which][:, a, :])
 
         q_in, q_codes, q_sc = {}, {}, {}
 
@@ -318,6 +351,7 @@ def tile_weighted_density_screened_poisson_k7_kernel(
             products(step)
             if not early_turn:
                 transposes(step)
+            spread(step)
 
         last = TILES - 1
         quantize_y(3, 0, 256, 384)

@@ -19,7 +19,9 @@ MULT = mybir.AluOpType.mult
 P = 128
 GROUPS = 2 * S
 TILES = 4 * S
-TAIL = 11
+SPLIT = 232
+SPLITS = {13: 64}
+SPREAD = [1, 2, 5, 7, 9, 11]
 
 
 def tile_weighted_density_screened_poisson_k7_kernel(
@@ -39,17 +41,24 @@ def tile_weighted_density_screened_poisson_k7_kernel(
         h_sc = keep.tile([P, GROUPS, NX], U8, name="h_sc", align_bytes=64)
         bg = keep.tile([P, GROUPS, 4], F32, name="bg", align_bytes=64)
         ident_bf = keep.tile([P, P], BF16, name="ident_bf", align_bytes=64)
+        bg_rows = keep.tile([P, 512], BF16, name="bg_rows", align_bytes=64)
         rows = keep.tile([P, NX], BF16, name="rows", align_bytes=64)
         ext_bc = keep.tile([P, S, NX], BF16, name="ext_bc", align_bytes=64)
         gain_bc = keep.tile([P, S, NX], BF16, name="gain_bc", align_bytes=64)
         y_codes = keep.tile([P, 2, S * J], U32, name="y_codes", align_bytes=64)
         y_sc = keep.tile([P, 2, S * J], U8, name="y_sc", align_bytes=64)
 
-        make_identity(nc, ident[:])
-        make_identity(nc, ident_bf[:])
-        nc.vector.memset(rows[:].bitcast(I32), 0)
+        nc.vector.memset(bg_rows[:].bitcast(I32), 0)
+        nc.vector.memset(ident[:], 0.0)
         nc.vector.memset(w_sc[:].rearrange("p a n -> p (a n)").bitcast(I32), 0)
-        nc.vector.memset(h_sc[:].rearrange("p a n -> p (a n)").bitcast(I32), 0)
+        nc.vector.memset(ident_bf[:], 0.0)
+        nc.vector.memset(rows[:].bitcast(I32), 0)
+        nc.vector.memset(h_sc[:, 0:2, :].rearrange("p a n -> p (a n)").bitcast(I32), 0)
+        nc.gpsimd.dma_start(out=bg_rows[0:GROUPS, :], in_=rho_bg.rearrange("a (g x) -> (a g) x", g=2))
+        make_identity(nc, ident[:], nomemset=True)
+        make_identity(nc, ident_bf[:], nomemset=True)
+        nc.gpsimd.dma_start(out=rows[0:S, :], in_=phi_ext)
+        nc.gpsimd.dma_start(out=rows[S : 2 * S, :], in_=gain)
 
         df = {}
 
@@ -74,46 +83,36 @@ def tile_weighted_density_screened_poisson_k7_kernel(
                 in_=src[g0:g1, :, :].rearrange("g p n -> p g n").bitcast(I32),
             )
 
-        nc.scalar.dma_start(out=rows[2 * S : 3 * S, :], in_=rho_bg)
-        load_scales(nc.scalar, w_sc, w_scales, 0, S)
-        nc.scalar.dma_start(out=rows[0:S, :], in_=phi_ext)
-        nc.scalar.dma_start(out=rows[S : 2 * S, :], in_=gain)
         load_df(0, 2)
+        load_df(1, 2)
+        load_scales(nc.sync, w_sc, w_scales, 0, S)
         load_words(w_sb, w_words, 0, 1)
-        load_df(1, 1)
         load_df(2, 1)
         load_scales(nc.sync, h_sc, h_scales, 0, 2)
         load_words(h_sb, h_words, 0, 2)
-        load_words(w_sb, w_words, 1, S)
         load_df(3, 1)
-        load_df(4, 1)
-        load_scales(nc.sync, h_sc, h_scales, 2, GROUPS)
+        load_words(w_sb, w_words, 1, S)
 
-        def late_loads(step):
-            if step == -7:
-                load_df(5, 1)
-                load_words(h_sb, h_words, 2, 4)
-            if step == -5:
-                load_df(6, 1)
-                load_words(h_sb, h_words, 4, 6)
-            if step == -3:
-                load_df(7, 1)
-                load_words(h_sb, h_words, 6, 8)
+        def late_loads():
+            nc.vector.memset(h_sc[:, 2:GROUPS, :].rearrange("p a n -> p (a n)").bitcast(I32), 0)
+            load_scales(nc.sync, h_sc, h_scales, 2, GROUPS)
+            load_df(4, 1)
+            load_words(h_sb, h_words, 2, 4)
+            load_df(5, 1)
+            load_df(6, 1)
+            load_words(h_sb, h_words, 4, 6)
+
+        def last_loads():
+            load_df(7, 1)
+            load_words(h_sb, h_words, 6, 8)
 
         def spread_background():
-            bank = psum.tile([P, 2, 4, S], F32, name="acc", bufs=6)
-            for g in range(2):
-                for t in range(4):
-                    nc.tensor.matmul(
-                        out=bank[:, g, t, :],
-                        lhsT=rows[:, 512 * g + t : 512 * (g + 1) : 4],
-                        rhs=ident_bf[:, 2 * S : 3 * S],
-                        start=True,
-                        stop=True,
-                    )
-            nc.scalar.copy(
-                out=bg[:].rearrange("p (a g) t -> p a g t", g=2), in_=bank[:].rearrange("p g t a -> p a g t")
-            )
+            bank = psum.tile([P, 4, GROUPS], F32, name="acc", bufs=6)
+            for t in range(4):
+                nc.tensor.matmul(
+                    out=bank[:, t, :], lhsT=bg_rows[:, t:512:4], rhs=ident_bf[:, 0:GROUPS], start=True, stop=True
+                )
+            nc.scalar.copy(out=bg[:], in_=bank[:].rearrange("p t h -> p h t"))
 
         def spread_row(r, dst):
             bank = psum.tile([P, NX], BF16, name="acc", bufs=6)
@@ -128,21 +127,20 @@ def tile_weighted_density_screened_poisson_k7_kernel(
                 )
             nc.scalar.copy(out=dst, in_=bank[:])
 
-        def spread(step):
-            if step == -8:
-                spread_background()
-            if -7 <= step < 1:
-                a, which = divmod(step + 7, 2)
-                spread_row(a + S * which, (ext_bc, gain_bc)[which][:, a, :])
+        def spread(n):
+            a, which = divmod(n, 2)
+            spread_row(a + S * which, (ext_bc, gain_bc)[which][:, a, :])
 
         q_in, q_codes, q_sc = {}, {}, {}
+        rho_banks, phi_banks, sums, ys, ybf, yt = {}, {}, {}, {}, {}, {}
 
         def staging(k):
             if k not in q_in:
-                q_in[k] = work.tile([P, 2, 2048], BF16, name="q_in", bufs=3, align_bytes=64)
+                q_in[k] = work.tile([P, 2, 1024], BF16, name="q_in", bufs=6, align_bytes=64)
             return q_in[k]
 
-        def turn_df(h, half):
+        def turn_df(n):
+            h, half = divmod(n, 2)
             bank = psum.tile([P, 2, 2, P], F32, name="turn", bufs=2)
             for tl in range(2):
                 words = df[h][:, 2 * half + tl, :].bitcast(F32)
@@ -150,61 +148,58 @@ def tile_weighted_density_screened_poisson_k7_kernel(
                     nc.tensor.transpose(bank[:, tl, u, :], words[:, u:256:2], ident[:])
             return bank
 
-        def copy_df(h, half, bank):
-            dst = staging(h - 2)[:, 0, 1024 * half : 1024 * (half + 1)].bitcast(F32)
+        def copy_df(n, bank):
+            dst = staging(n - 5)[:, 0, :].bitcast(F32)
             nc.scalar.copy(
                 out=dst.rearrange("p (t r u) -> p t r u", t=2, u=2),
                 in_=bank[:].rearrange("p t u r -> p t r u"),
             )
 
-        def quantize_pair(k):
-            q_codes[k] = work.tile([P, 2, 512], U32, name="q_codes", bufs=5, align_bytes=64)
-            q_sc[k] = work.tile([P, 2, 512], U8, name="q_sc", bufs=5, align_bytes=64)
-            lo = 0 if k + 2 < GROUPS else 1
-            hi = 2 if k >= 0 else 1
+        def quantize_operands(k, lo, hi):
+            if k not in q_codes:
+                q_codes[k] = work.tile([P, 2, 256], U32, name="q_codes", bufs=9, align_bytes=64)
+                q_sc[k] = work.tile([P, 2, 256], U8, name="q_sc", bufs=9, align_bytes=64)
             nc.vector.quantize_mx(
                 out=q_codes[k][:, lo:hi, :].rearrange("p s n -> p (s n)").bitcast(FP8X4),
                 scales=q_sc[k][:, lo:hi, :].rearrange("p s n -> p (s n)"),
                 in_=q_in[k][:, lo:hi, :].rearrange("p s n -> p (s n)"),
             )
 
-        rho_banks, phi_banks, sums, ys, ybf, yt = {}, {}, {}, {}, {}, {}
-
-        def density(h, jc):
-            a = h // 2
+        def density(s, g):
+            a, jt = divmod(s, 4)
             bank = psum.tile([P, 512], F32, name="acc", bufs=6)
-            rho_banks[h, jc] = bank
+            rho_banks[s, g] = bank
             for t in range(4):
-                cols = slice(P * t, P * (t + 1))
+                k = 4 * a + 2 * g + t // 2 - 5
+                cols = slice(P * (t % 2), P * (t % 2 + 1))
                 nc.tensor.matmul_mx(
-                    out=bank[:, cols],
-                    lhsT=q_codes[h - 2][:, 0, cols].bitcast(FP8X4),
-                    lhsT_scale=q_sc[h - 2][:, 0, cols],
-                    rhs=w_sb[:, a, 2 * P * jc : 2 * P * (jc + 1)].bitcast(FP4X4),
-                    rhs_scale=w_sc[:, a, P * jc : P * (jc + 1)],
+                    out=bank[:, P * t : P * (t + 1)],
+                    lhsT=q_codes[k][:, 0, cols].bitcast(FP8X4),
+                    lhsT_scale=q_sc[k][:, 0, cols],
+                    rhs=w_sb[:, a, 2 * P * jt : 2 * P * (jt + 1)].bitcast(FP4X4),
+                    rhs_scale=w_sc[:, a, P * jt : P * (jt + 1)],
                     start=True,
                     stop=True,
                 )
 
-        def add_background(h, jc):
+        def add_background(s, g):
             nc.vector.tensor_tensor(
-                out=staging(h)[:, 1, 512 * jc : 512 * (jc + 1)].rearrange("p (n t) -> p n t", t=4),
-                in0=rho_banks[h, jc][:].rearrange("p (t n) -> p n t", t=4),
-                in1=bg[:, h, :].unsqueeze(1).to_broadcast([P, P, 4]),
+                out=staging(s)[:, 1, 512 * g : 512 * (g + 1)].rearrange("p (n t) -> p n t", t=4),
+                in0=rho_banks[s, g][:].rearrange("p (t n) -> p n t", t=4),
+                in1=bg[:, 2 * (s // 4) + g, :].unsqueeze(1).to_broadcast([P, P, 4]),
                 op=ADD,
             )
 
         def potential(s, zh):
-            a, jt = divmod(s, 4)
             bank = psum.tile([P, 512], F32, name="acc", bufs=6)
             phi_banks[s, zh] = bank
-            cols = slice(P * jt, P * (jt + 1))
             for g in range(2):
-                h = 2 * a + g
+                h = 2 * (s // 4) + g
+                cols = slice(P * g, P * (g + 1))
                 nc.tensor.matmul_mx(
                     out=bank[:],
-                    lhsT=q_codes[h][:, 1, cols].bitcast(FP8X4),
-                    lhsT_scale=q_sc[h][:, 1, cols],
+                    lhsT=q_codes[s][:, 1, cols].bitcast(FP8X4),
+                    lhsT_scale=q_sc[s][:, 1, cols],
                     rhs=h_sb[:, h, 1024 * zh : 1024 * (zh + 1)].bitcast(FP4X4),
                     rhs_scale=h_sc[:, h, 512 * zh : 512 * (zh + 1)],
                     start=(g == 0),
@@ -212,17 +207,15 @@ def tile_weighted_density_screened_poisson_k7_kernel(
                 )
 
         def add_external(s, zh):
-            a = s // 4
             if zh == 0:
                 sums[s] = work.tile([P, NX], F32, name="sums", bufs=3, align_bytes=64)
             cols = slice(512 * zh, 512 * (zh + 1))
-            nc.vector.tensor_tensor(out=sums[s][:, cols], in0=phi_banks[s, zh][:], in1=ext_bc[:, a, cols], op=ADD)
+            nc.vector.tensor_tensor(out=sums[s][:, cols], in0=phi_banks[s, zh][:], in1=ext_bc[:, s // 4, cols], op=ADD)
 
         def apply_gain(s, z0, z1, engine):
-            a = s // 4
             if z0 == 0:
-                ys[s] = work.tile([P, NX], F32, name="y", bufs=10, align_bytes=64)
-            engine.tensor_tensor(out=ys[s][:, z0:z1], in0=sums[s][:, z0:z1], in1=gain_bc[:, a, z0:z1], op=MULT)
+                ys[s] = work.tile([P, NX], F32, name="y", bufs=8, align_bytes=64)
+            engine.tensor_tensor(out=ys[s][:, z0:z1], in0=sums[s][:, z0:z1], in1=gain_bc[:, s // 4, z0:z1], op=MULT)
 
         def store_y(s, z0, z1):
             a, jt = divmod(s, 4)
@@ -243,25 +236,26 @@ def tile_weighted_density_screened_poisson_k7_kernel(
                     nc.tensor.transpose(bank[:, zh, u, :], words, ident[:])
             return bank
 
-        def copy_y(s, halves, bank):
-            a, jt = divmod(s, 4)
-            if a not in yt:
-                yt[a] = work.tile([P, 2, 2048], BF16, name="yt", bufs=2, align_bytes=64)
+        def copy_y(s, halves, bank, copy=nc.scalar.copy):
+            pair, i = divmod(s, 2)
+            if pair not in yt:
+                yt[pair] = work.tile([P, 2, 1024], BF16, name="yt", bufs=4, align_bytes=64)
             g0, g1 = halves[0], halves[-1] + 1
-            dst = yt[a][:, g0:g1, 512 * jt : 512 * (jt + 1)].bitcast(F32)
-            nc.scalar.copy(
+            dst = yt[pair][:, g0:g1, 512 * i : 512 * (i + 1)].bitcast(F32)
+            copy(
                 out=dst.rearrange("p g (r u) -> p g r u", u=2),
                 in_=bank[:, g0:g1, :, :].rearrange("p g u r -> p g r u"),
             )
 
-        def quantize_y(a, g, j0, j1):
-            cols = slice(J * a + j0, J * a + j1)
-            nc.vector.quantize_mx(
-                out=y_codes[:, g, cols].bitcast(FP8X4), scales=y_sc[:, g, cols], in_=yt[a][:, g, 4 * j0 : 4 * j1]
-            )
+        def quantize_y(pair, g):
+            cols = slice(256 * pair, 256 * (pair + 1))
+            nc.vector.quantize_mx(out=y_codes[:, g, cols].bitcast(FP8X4), scales=y_sc[:, g, cols], in_=yt[pair][:, g, :])
+
+        def store_words(pair, g0, g1):
+            cols = slice(256 * pair, 256 * (pair + 1))
             nc.sync.dma_start(
-                out=out_1[g, :, cols, :].rearrange("p m t -> p (m t)").bitcast(I32),
-                in_=y_codes[:, g, cols].bitcast(I32),
+                out=out_1[g0:g1, :, cols, :].rearrange("g p m t -> p g (m t)").bitcast(I32),
+                in_=y_codes[:, g0:g1, cols].bitcast(I32),
             )
 
         def store_scales(engines, m0, m1):
@@ -271,96 +265,119 @@ def tile_weighted_density_screened_poisson_k7_kernel(
                     in_=y_sc[32 * q : 32 * q + 4, :, m0:m1].bitcast(I32),
                 )
 
-        def quantize_step(step):
-            if step % 2 and -2 <= (step + 3) // 2 < GROUPS:
-                quantize_pair((step + 3) // 2)
-            if step in (6, 10, 13):
-                quantize_y((step - 5) // 4, 0, 0, J)
-            if step in (8, 12, 14):
-                quantize_y((step - 6) // 4 if step > 8 else 0, 1, 0, J)
-            if step == 15:
-                store_scales([nc.sync], 0, 3 * J)
-                quantize_y(3, 0, 0, 256)
-                quantize_y(3, 1, 0, 256)
+        def prepare(n):
+            copy_df(n, turn_df(n))
 
-        def transposes(step):
-            h, half = divmod(step + 9, 2)
-            jobs = []
-            if h < GROUPS:
-                jobs.append((copy_df, h, half, turn_df(h, half)))
-            todo = []
-            if 0 <= step - 2 and step <= TAIL + 1:
-                todo.append(step - 2)
-            if TAIL + 1 <= step:
-                todo.append(step - 1)
-            for s in todo:
-                jobs.append((copy_y, s, (0, 1), turn_y(s, (0, 1))))
-            for fn, x, part, bank in jobs:
-                fn(x, part, bank)
-
-        def products(step):
-            nxt = step + 1
-            h, first = divmod(nxt + 5, 2)
-            for i in range(2):
-                if 0 <= nxt < TILES:
-                    potential(nxt, i)
-                if 0 <= h < GROUPS:
-                    density(h, 2 * first + i)
-
-        for step in range(-9, TILES):
-            late_loads(step)
-            if step >= 1:
-                round_y(step - 1, 0)
-                round_y(step - 1, 1)
-                store_y(step - 1, 0, NX)
-            early_turn = -4 < step <= TAIL
-            if early_turn:
-                transposes(step)
-            h, first = divmod(step + 5, 2)
-            has_rho = 0 <= h < GROUPS
-            if step == TILES - 1:
-                add_external(step, 0)
-                add_external(step, 1)
-                apply_gain(step, 0, 512, nc.vector)
-                apply_gain(step, 512, NX, nc.vector)
-                quantize_step(step)
-            elif step >= TAIL:
-                add_external(step, 0)
-                add_external(step, 1)
-                apply_gain(step, 0, 520, nc.vector)
-                apply_gain(step, 512, NX, nc.gpsimd)
-                quantize_step(step)
-            elif step >= 0:
-                add_external(step, 0)
-                apply_gain(step, 0, 512, nc.gpsimd)
-                quantize_step(step)
-                add_background(h, 2 * first)
-                add_external(step, 1)
-                apply_gain(step, 512, NX, nc.gpsimd)
-                add_background(h, 2 * first + 1)
-            elif step == -5:
-                add_background(h, 0)
-                add_background(h, 1)
-                quantize_step(step)
-            else:
-                if has_rho:
-                    add_background(h, 2 * first)
-                quantize_step(step)
-                if has_rho:
-                    add_background(h, 2 * first + 1)
-            products(step)
-            if not early_turn:
-                transposes(step)
-            spread(step)
+        prepare(0)
+        prepare(1)
+        late_loads()
+        quantize_operands(-5, 0, 1)
+        quantize_operands(-4, 0, 1)
+        prepare(2)
+        prepare(3)
+        spread_background()
+        density(0, 0)
+        density(1, 0)
+        last_loads()
+        quantize_operands(-3, 0, 1)
+        add_background(0, 0)
+        quantize_operands(-2, 0, 1)
+        add_background(1, 0)
+        prepare(4)
+        prepare(5)
+        density(0, 1)
+        density(1, 1)
+        density(2, 0)
+        spread(0)
+        prepare(6)
+        add_background(0, 1)
+        quantize_operands(-1, 0, 1)
 
         last = TILES - 1
-        quantize_y(3, 0, 256, 384)
-        quantize_y(3, 1, 256, 384)
-        for zh in range(2):
-            round_y(last, zh)
-            store_y(last, 512 * zh, 512 * (zh + 1))
-        for zh in range(2):
-            copy_y(last, (zh,), turn_y(last, (zh,)))
-        for zh in range(2):
-            quantize_y(3, zh, 384, 512)
-        store_scales([nc.scalar, nc.sync], 3 * J, 4 * J)
+        both = (0, 1)
+        for step in range(last - 1):
+            if step >= 2:
+                round_y(step - 2, 0)
+                round_y(step - 2, 1)
+                store_y(step - 2, 0, NX)
+            quantize_operands(step, 0 if step < TILES - 5 else 1, 2)
+            if 5 <= step:
+                pair, g = divmod(step - 5, 2)
+                quantize_y(pair, g)
+                if g == 1:
+                    store_words(pair, 0, 2)
+            if step >= 1:
+                split = SPLITS.get(step, SPLIT)
+                apply_gain(step - 1, 0, split, nc.vector)
+                apply_gain(step - 1, split - 8, NX, nc.gpsimd)
+            potential(step, 0)
+            potential(step, 1)
+            if step == 0:
+                spread(1)
+            add_background(step + 1, 1)
+            add_background(step + 2, 0)
+            if step + 2 == last:
+                add_background(last, 1)
+            add_external(step, 0)
+            add_external(step, 1)
+            if step + 2 < last:
+                density(step + 2, 1)
+            if step + 3 < TILES:
+                density(step + 3, 0)
+            if step + 3 == last:
+                density(last, 1)
+            if step in SPREAD:
+                spread(2 + SPREAD.index(step))
+            jobs = []
+            if step + 7 < TILES:
+                jobs.append((turn_df(step + 7), None))
+            if step >= 2:
+                jobs.append((turn_y(step - 2, both), step - 2))
+            for bank, s in jobs:
+                if s is None:
+                    copy_df(step + 7, bank)
+                else:
+                    copy_y(s, both, bank)
+
+        round_y(12, 0)
+        round_y(12, 1)
+        store_y(12, 0, NX)
+        quantize_operands(14, 1, 2)
+        quantize_operands(15, 1, 2)
+        quantize_y(4, 1)
+        store_words(4, 0, 2)
+        quantize_y(5, 0)
+        quantize_y(5, 1)
+        store_words(5, 0, 2)
+        store_scales([nc.sync], 0, 6 * 256)
+        apply_gain(13, 0, 400, nc.vector)
+        apply_gain(13, 400 - 8, NX, nc.gpsimd)
+        for s in (14, 15):
+            potential(s, 0)
+            potential(s, 1)
+        copy_y(12, both, turn_y(12, both))
+        for s in (14, 15):
+            add_external(s, 0)
+            add_external(s, 1)
+        round_y(13, 0)
+        round_y(13, 1)
+        store_y(13, 0, NX)
+        for s in (14, 15):
+            for zh in both:
+                apply_gain(s, 512 * zh, 512 * (zh + 1), nc.vector)
+                round_y(s, zh)
+                if s == last:
+                    store_y(s, 512 * zh, 512 * (zh + 1))
+            if s < last:
+                store_y(s, 0, NX)
+        copy_y(13, both, turn_y(13, both), nc.vector.tensor_copy)
+        copy_y(14, both, turn_y(14, both), nc.vector.tensor_copy)
+        quantize_y(6, 0)
+        quantize_y(6, 1)
+        store_words(6, 0, 2)
+        for zh in both:
+            copy_y(15, (zh,), turn_y(15, (zh,)))
+        for zh in both:
+            quantize_y(7, zh)
+            store_words(7, zh, zh + 1)
+        store_scales([nc.scalar, nc.sync], 6 * 256, 8 * 256)

from contextlib import ExitStack

import concourse.mybir as mybir
from concourse.masks import make_identity

S, NX, NV, J = 4, 1024, 512, 512
FLOPS = 2 * S * NX * NV * J + 2 * S * J * NX * NX

F32 = mybir.dt.float32
BF16 = mybir.dt.bfloat16
I32 = mybir.dt.int32
U32 = mybir.dt.uint32
U8 = mybir.dt.uint8
FP8X4 = mybir.dt.float8_e4m3fn_x4
FP4X4 = mybir.dt.float4_e2m1fn_x4
ADD = mybir.AluOpType.add
MULT = mybir.AluOpType.mult

P = 128
GROUPS = 2 * S
TILES = 4 * S
SPLIT = 232
SPLITS = {13: 64}
SPREAD = [1, 2, 5, 7, 9, 11]


def tile_weighted_density_screened_poisson_k7_kernel(
    tc, delta_f, w_words, w_scales, rho_bg, h_words, h_scales, phi_ext, gain, out_0, out_1, out_2
):
    nc = tc.nc
    with ExitStack() as ctx:
        keep = ctx.enter_context(tc.tile_pool(name="keep", bufs=1))
        work = ctx.enter_context(tc.tile_pool(name="work", bufs=2))
        psum = ctx.enter_context(tc.psum_pool(name="psum", bufs=2))
        ctx.enter_context(tc.manual_schedule())

        ident = keep.tile([P, P], F32, name="ident", align_bytes=64)
        w_sb = keep.tile([P, S, 2 * J], U8, name="w_sb", align_bytes=64)
        w_sc = keep.tile([P, S, J], U8, name="w_sc", align_bytes=64)
        h_sb = keep.tile([P, GROUPS, 2 * NX], U8, name="h_sb", align_bytes=64)
        h_sc = keep.tile([P, GROUPS, NX], U8, name="h_sc", align_bytes=64)
        bg = keep.tile([P, GROUPS, 4], F32, name="bg", align_bytes=64)
        ident_bf = keep.tile([P, P], BF16, name="ident_bf", align_bytes=64)
        bg_rows = keep.tile([P, 512], BF16, name="bg_rows", align_bytes=64)
        rows = keep.tile([P, NX], BF16, name="rows", align_bytes=64)
        ext_bc = keep.tile([P, S, NX], BF16, name="ext_bc", align_bytes=64)
        gain_bc = keep.tile([P, S, NX], BF16, name="gain_bc", align_bytes=64)
        y_codes = keep.tile([P, 2, S * J], U32, name="y_codes", align_bytes=64)
        y_sc = keep.tile([P, 2, S * J], U8, name="y_sc", align_bytes=64)

        nc.vector.memset(bg_rows[:].bitcast(I32), 0)
        nc.vector.memset(ident[:], 0.0)
        nc.vector.memset(w_sc[:].rearrange("p a n -> p (a n)").bitcast(I32), 0)
        nc.vector.memset(ident_bf[:], 0.0)
        nc.vector.memset(rows[:].bitcast(I32), 0)
        nc.vector.memset(h_sc[:, 0:2, :].rearrange("p a n -> p (a n)").bitcast(I32), 0)
        nc.gpsimd.dma_start(out=bg_rows[0:GROUPS, :], in_=rho_bg.rearrange("a (g x) -> (a g) x", g=2))
        make_identity(nc, ident[:], nomemset=True)
        make_identity(nc, ident_bf[:], nomemset=True)
        nc.gpsimd.dma_start(out=rows[0:S, :], in_=phi_ext)
        nc.gpsimd.dma_start(out=rows[S : 2 * S, :], in_=gain)

        df = {}

        def load_df(h, pieces):
            a, g = divmod(h, 2)
            df[h] = work.tile([P, 4, NV], BF16, name="df", bufs=5, align_bytes=64)
            src = delta_f[a, 512 * g : 512 * (g + 1), :].rearrange("(p t) v -> p t v", t=4)
            step = 4 // pieces
            for t0 in range(0, 4, step):
                nc.sync.dma_start(out=df[h][:, t0 : t0 + step, :], in_=src[:, t0 : t0 + step, :])

        def load_scales(engine, plane, src, g0, g1):
            for q in range(4):
                engine.dma_start(
                    out=plane[32 * q : 32 * q + 4, g0:g1, :].bitcast(I32),
                    in_=src[g0:g1, 4 * q : 4 * q + 4, :].rearrange("g r n -> r g n").bitcast(I32),
                )

        def load_words(dst, src, g0, g1):
            nc.sync.dma_start(
                out=dst[:, g0:g1, :].bitcast(I32),
                in_=src[g0:g1, :, :].rearrange("g p n -> p g n").bitcast(I32),
            )

        load_df(0, 2)
        load_df(1, 2)
        load_scales(nc.sync, w_sc, w_scales, 0, S)
        load_words(w_sb, w_words, 0, 1)
        load_df(2, 1)
        load_scales(nc.sync, h_sc, h_scales, 0, 2)
        load_words(h_sb, h_words, 0, 2)
        load_df(3, 1)
        load_words(w_sb, w_words, 1, S)

        def late_loads():
            nc.vector.memset(h_sc[:, 2:GROUPS, :].rearrange("p a n -> p (a n)").bitcast(I32), 0)
            load_scales(nc.sync, h_sc, h_scales, 2, GROUPS)
            load_df(4, 1)
            load_words(h_sb, h_words, 2, 4)
            load_df(5, 1)
            load_df(6, 1)
            load_words(h_sb, h_words, 4, 6)

        def last_loads():
            load_df(7, 1)
            load_words(h_sb, h_words, 6, 8)

        def spread_background():
            bank = psum.tile([P, 4, GROUPS], F32, name="acc", bufs=6)
            for t in range(4):
                nc.tensor.matmul(
                    out=bank[:, t, :], lhsT=bg_rows[:, t:512:4], rhs=ident_bf[:, 0:GROUPS], start=True, stop=True
                )
            nc.scalar.copy(out=bg[:], in_=bank[:].rearrange("p t h -> p h t"))

        def spread_row(r, dst):
            bank = psum.tile([P, NX], BF16, name="acc", bufs=6)
            for zh in range(2):
                cols = slice(512 * zh, 512 * (zh + 1))
                nc.tensor.matmul(
                    out=bank[:, cols],
                    lhsT=ident_bf[:, r : r + 1].to_broadcast([P, P]),
                    rhs=rows[:, cols],
                    start=True,
                    stop=True,
                )
            nc.scalar.copy(out=dst, in_=bank[:])

        def spread(n):
            a, which = divmod(n, 2)
            spread_row(a + S * which, (ext_bc, gain_bc)[which][:, a, :])

        q_in, q_codes, q_sc = {}, {}, {}
        rho_banks, phi_banks, sums, ys, ybf, yt = {}, {}, {}, {}, {}, {}

        def staging(k):
            if k not in q_in:
                q_in[k] = work.tile([P, 2, 1024], BF16, name="q_in", bufs=6, align_bytes=64)
            return q_in[k]

        def turn_df(n):
            h, half = divmod(n, 2)
            bank = psum.tile([P, 2, 2, P], F32, name="turn", bufs=2)
            for tl in range(2):
                words = df[h][:, 2 * half + tl, :].bitcast(F32)
                for u in range(2):
                    nc.tensor.transpose(bank[:, tl, u, :], words[:, u:256:2], ident[:])
            return bank

        def copy_df(n, bank):
            dst = staging(n - 5)[:, 0, :].bitcast(F32)
            nc.scalar.copy(
                out=dst.rearrange("p (t r u) -> p t r u", t=2, u=2),
                in_=bank[:].rearrange("p t u r -> p t r u"),
            )

        def quantize_operands(k, lo, hi):
            if k not in q_codes:
                q_codes[k] = work.tile([P, 2, 256], U32, name="q_codes", bufs=9, align_bytes=64)
                q_sc[k] = work.tile([P, 2, 256], U8, name="q_sc", bufs=9, align_bytes=64)
            nc.vector.quantize_mx(
                out=q_codes[k][:, lo:hi, :].rearrange("p s n -> p (s n)").bitcast(FP8X4),
                scales=q_sc[k][:, lo:hi, :].rearrange("p s n -> p (s n)"),
                in_=q_in[k][:, lo:hi, :].rearrange("p s n -> p (s n)"),
            )

        def density(s, g):
            a, jt = divmod(s, 4)
            bank = psum.tile([P, 512], F32, name="acc", bufs=6)
            rho_banks[s, g] = bank
            for t in range(4):
                k = 4 * a + 2 * g + t // 2 - 5
                cols = slice(P * (t % 2), P * (t % 2 + 1))
                nc.tensor.matmul_mx(
                    out=bank[:, P * t : P * (t + 1)],
                    lhsT=q_codes[k][:, 0, cols].bitcast(FP8X4),
                    lhsT_scale=q_sc[k][:, 0, cols],
                    rhs=w_sb[:, a, 2 * P * jt : 2 * P * (jt + 1)].bitcast(FP4X4),
                    rhs_scale=w_sc[:, a, P * jt : P * (jt + 1)],
                    start=True,
                    stop=True,
                )

        def add_background(s, g):
            nc.vector.tensor_tensor(
                out=staging(s)[:, 1, 512 * g : 512 * (g + 1)].rearrange("p (n t) -> p n t", t=4),
                in0=rho_banks[s, g][:].rearrange("p (t n) -> p n t", t=4),
                in1=bg[:, 2 * (s // 4) + g, :].unsqueeze(1).to_broadcast([P, P, 4]),
                op=ADD,
            )

        def potential(s, zh):
            bank = psum.tile([P, 512], F32, name="acc", bufs=6)
            phi_banks[s, zh] = bank
            for g in range(2):
                h = 2 * (s // 4) + g
                cols = slice(P * g, P * (g + 1))
                nc.tensor.matmul_mx(
                    out=bank[:],
                    lhsT=q_codes[s][:, 1, cols].bitcast(FP8X4),
                    lhsT_scale=q_sc[s][:, 1, cols],
                    rhs=h_sb[:, h, 1024 * zh : 1024 * (zh + 1)].bitcast(FP4X4),
                    rhs_scale=h_sc[:, h, 512 * zh : 512 * (zh + 1)],
                    start=(g == 0),
                    stop=(g == 1),
                )

        def add_external(s, zh):
            if zh == 0:
                sums[s] = work.tile([P, NX], F32, name="sums", bufs=3, align_bytes=64)
            cols = slice(512 * zh, 512 * (zh + 1))
            nc.vector.tensor_tensor(out=sums[s][:, cols], in0=phi_banks[s, zh][:], in1=ext_bc[:, s // 4, cols], op=ADD)

        def apply_gain(s, z0, z1, engine):
            if z0 == 0:
                ys[s] = work.tile([P, NX], F32, name="y", bufs=8, align_bytes=64)
            engine.tensor_tensor(out=ys[s][:, z0:z1], in0=sums[s][:, z0:z1], in1=gain_bc[:, s // 4, z0:z1], op=MULT)

        def store_y(s, z0, z1):
            a, jt = divmod(s, 4)
            nc.sync.dma_start(out=out_0[a, P * jt : P * (jt + 1), z0:z1], in_=ys[s][:, z0:z1])

        def round_y(s, zh):
            ybf[s, zh] = work.tile([P, 2, P, 2], BF16, name="ybf", bufs=6, align_bytes=64)
            nc.scalar.copy(
                out=ybf[s, zh][:],
                in_=ys[s][:, 512 * zh : 512 * (zh + 1)].rearrange("p (m u e) -> p u m e", u=2, e=2),
            )

        def turn_y(s, halves):
            bank = psum.tile([P, 2, 2, P], F32, name="turn", bufs=2)
            for zh in halves:
                for u in range(2):
                    words = ybf[s, zh][:, u, :, :].rearrange("p m e -> p (m e)").bitcast(F32)
                    nc.tensor.transpose(bank[:, zh, u, :], words, ident[:])
            return bank

        def copy_y(s, halves, bank, copy=nc.scalar.copy):
            pair, i = divmod(s, 2)
            if pair not in yt:
                yt[pair] = work.tile([P, 2, 1024], BF16, name="yt", bufs=4, align_bytes=64)
            g0, g1 = halves[0], halves[-1] + 1
            dst = yt[pair][:, g0:g1, 512 * i : 512 * (i + 1)].bitcast(F32)
            copy(
                out=dst.rearrange("p g (r u) -> p g r u", u=2),
                in_=bank[:, g0:g1, :, :].rearrange("p g u r -> p g r u"),
            )

        def quantize_y(pair, g):
            cols = slice(256 * pair, 256 * (pair + 1))
            nc.vector.quantize_mx(out=y_codes[:, g, cols].bitcast(FP8X4), scales=y_sc[:, g, cols], in_=yt[pair][:, g, :])

        def store_words(pair, g0, g1):
            cols = slice(256 * pair, 256 * (pair + 1))
            nc.sync.dma_start(
                out=out_1[g0:g1, :, cols, :].rearrange("g p m t -> p g (m t)").bitcast(I32),
                in_=y_codes[:, g0:g1, cols].bitcast(I32),
            )

        def store_scales(engines, m0, m1):
            for q in range(4):
                engines[q % len(engines)].dma_start(
                    out=out_2[:, 4 * q : 4 * q + 4, m0:m1].rearrange("g r m -> r g m").bitcast(I32),
                    in_=y_sc[32 * q : 32 * q + 4, :, m0:m1].bitcast(I32),
                )

        def prepare(n):
            copy_df(n, turn_df(n))

        prepare(0)
        prepare(1)
        late_loads()
        quantize_operands(-5, 0, 1)
        quantize_operands(-4, 0, 1)
        prepare(2)
        prepare(3)
        spread_background()
        density(0, 0)
        density(1, 0)
        last_loads()
        quantize_operands(-3, 0, 1)
        add_background(0, 0)
        quantize_operands(-2, 0, 1)
        add_background(1, 0)
        prepare(4)
        prepare(5)
        density(0, 1)
        density(1, 1)
        density(2, 0)
        spread(0)
        prepare(6)
        add_background(0, 1)
        quantize_operands(-1, 0, 1)

        last = TILES - 1
        both = (0, 1)
        for step in range(last - 1):
            if step >= 2:
                round_y(step - 2, 0)
                round_y(step - 2, 1)
                store_y(step - 2, 0, NX)
            quantize_operands(step, 0 if step < TILES - 5 else 1, 2)
            if 5 <= step:
                pair, g = divmod(step - 5, 2)
                quantize_y(pair, g)
                if g == 1:
                    store_words(pair, 0, 2)
            if step >= 1:
                split = SPLITS.get(step, SPLIT)
                apply_gain(step - 1, 0, split, nc.vector)
                apply_gain(step - 1, split - 8, NX, nc.gpsimd)
            potential(step, 0)
            potential(step, 1)
            if step == 0:
                spread(1)
            add_background(step + 1, 1)
            add_background(step + 2, 0)
            if step + 2 == last:
                add_background(last, 1)
            add_external(step, 0)
            add_external(step, 1)
            if step + 2 < last:
                density(step + 2, 1)
            if step + 3 < TILES:
                density(step + 3, 0)
            if step + 3 == last:
                density(last, 1)
            if step in SPREAD:
                spread(2 + SPREAD.index(step))
            jobs = []
            if step + 7 < TILES:
                jobs.append((turn_df(step + 7), None))
            if step >= 2:
                jobs.append((turn_y(step - 2, both), step - 2))
            for bank, s in jobs:
                if s is None:
                    copy_df(step + 7, bank)
                else:
                    copy_y(s, both, bank)

        round_y(12, 0)
        round_y(12, 1)
        store_y(12, 0, NX)
        quantize_operands(14, 1, 2)
        quantize_operands(15, 1, 2)
        quantize_y(4, 1)
        store_words(4, 0, 2)
        quantize_y(5, 0)
        quantize_y(5, 1)
        store_words(5, 0, 2)
        store_scales([nc.sync], 0, 6 * 256)
        apply_gain(13, 0, 400, nc.vector)
        apply_gain(13, 400 - 8, NX, nc.gpsimd)
        for s in (14, 15):
            potential(s, 0)
            potential(s, 1)
        copy_y(12, both, turn_y(12, both))
        for s in (14, 15):
            add_external(s, 0)
            add_external(s, 1)
        round_y(13, 0)
        round_y(13, 1)
        store_y(13, 0, NX)
        for s in (14, 15):
            for zh in both:
                apply_gain(s, 512 * zh, 512 * (zh + 1), nc.vector)
                round_y(s, zh)
                if s == last:
                    store_y(s, 512 * zh, 512 * (zh + 1))
            if s < last:
                store_y(s, 0, NX)
        copy_y(13, both, turn_y(13, both), nc.vector.tensor_copy)
        copy_y(14, both, turn_y(14, both), nc.vector.tensor_copy)
        quantize_y(6, 0)
        quantize_y(6, 1)
        store_words(6, 0, 2)
        for zh in both:
            copy_y(15, (zh,), turn_y(15, (zh,)))
        for zh in both:
            quantize_y(7, zh)
            store_words(7, zh, zh + 1)
        store_scales([nc.scalar, nc.sync], 6 * 256, 8 * 256)
